import numpy as np
import ml_dtypes


def mxq(x, axis, fmt="e4m3"):
    dtype, down = {"e4m3": (ml_dtypes.float8_e4m3fn, 7), "e5m2": (ml_dtypes.float8_e5m2, 14)}[fmt]
    v = np.moveaxis(np.asarray(x, np.float32).astype(ml_dtypes.bfloat16).astype(np.float64), axis, -1)
    blocks = v.reshape(v.shape[:-1] + (-1, 32))
    amax = np.abs(blocks).max(-1, keepdims=True)
    byte = np.maximum(np.where(amax > 0, np.frexp(amax)[1] - 1 + 127, 0) - down, 1)
    scale = np.exp2(byte - 127.0)
    codes = (blocks / scale).astype(np.float32).astype(dtype).astype(np.float64)
    return np.moveaxis((codes * scale).reshape(v.shape), -1, axis)


WIDE = False


def mx_kscale(k):
    if not WIDE:
        return np.ones(k)
    levels = np.array([10, -10, 5, -5, 0])
    if k % 512:
        return np.exp2(np.random.permutation(np.resize(levels, k // 32))).repeat(32)
    a = np.empty((k // 512, 16))
    for p in range(k // 512):
        a[p, :8] = np.random.permutation(np.resize(levels, 8))
        for g in range(8):
            far = levels[np.abs(levels - a[p, g]) >= 10]
            a[p, g + 8] = far[np.random.randint(len(far))]
    return np.exp2(a.ravel()).repeat(32)


def f64(x):
    return np.asarray(x).astype(np.float64)


def striped(idx):
    return np.tile(idx.reshape(-1, 16).T, (8, 1)).astype(np.uint16)


def unstriped(offs):
    return offs[:16].T.reshape(-1).astype(np.int64)


def striped8(idx):
    return np.concatenate([x.reshape(-1, 16).T for x in idx]).astype(np.uint16)


def runs(offs, k):
    lists = np.stack([offs[16 * r : 16 * r + 16].T.reshape(-1) for r in range(8)]).astype(np.int64)
    return lists[np.arange(k) % 512 // 64]


def pack_weight(w):
    k, n = w.shape
    w = f64(np.asarray(w, np.float32).astype(ml_dtypes.bfloat16)).reshape(k // 32, 32, n)
    amax = np.abs(w).max(1)
    byte = np.clip(np.where(amax > 0, np.frexp(amax)[1] - 1 + 127 - 7, 1), 1, 254)
    scaled = (w * np.exp2(127.0 - byte)[:, None, :]).reshape(k, n).astype(np.float32)
    words = np.ascontiguousarray(scaled.reshape(k // 512, 128, 4, n).transpose(0, 1, 3, 2)).astype(ml_dtypes.float8_e4m3fn).view(np.uint8)
    return words, np.ascontiguousarray(byte.astype(np.uint8).reshape(k // 512, 16, n))


def unpack_weight(words, scales):
    g, p, n, _ = words.shape
    vals = np.ascontiguousarray(words).view(ml_dtypes.float8_e4m3fn).astype(np.float64) * np.repeat(np.exp2(scales.astype(np.float64) - 127.0), 8, axis=1)[..., None]
    return vals.transpose(0, 1, 3, 2).reshape(g * 512, n)


def sigmoid(v):
    return 1.0 / (1.0 + np.exp(-np.maximum(v, -700.0)))

def planes(y):
    n, m = y.shape
    v = y.astype(np.float32).astype(ml_dtypes.bfloat16).astype(np.float64).reshape(n // 32, 32, m)
    top = np.abs(v).max(1)
    byte = np.clip(np.where(top > 0, np.frexp(top)[1] - 1 + 127 - 7, 1), 1, 254)
    codes = (v * np.exp2(127.0 - byte)[:, None, :]).reshape(n, m).astype(np.float32).astype(ml_dtypes.float8_e4m3fn).view(np.uint8)
    words = codes.reshape(n // 512, 128, 4, m).transpose(0, 1, 3, 2)
    return np.ascontiguousarray(words), np.ascontiguousarray(byte.astype(np.uint8).reshape(n // 512, 16, m))


K, T, S, N, G, H = 512, 1024, 512, 512, 2048, 512


def setup_inputs():
    n = np.random.standard_normal
    s = mx_kscale(K)[:, None]
    u = mx_kscale(S)
    packed_xT = pack_weight(n((K, T)) * s)
    packed_dT = pack_weight(n((K, G)) / s)
    packed_w1 = pack_weight(n((H, N)) / np.sqrt(2 * H) / u[:, None])
    packed_w2 = pack_weight(n((H, N)) / np.sqrt(2 * H) / u[:, None])
    return {
        "x_words": packed_xT[0],
        "x_scales": packed_xT[1],
        "d_words": packed_dT[0],
        "d_scales": packed_dT[1],
        "gn": (np.random.uniform(0.5, 1.5, (H, 1)) * u[:, None]).astype(np.float32),
        "gm": (np.random.uniform(0.5, 1.5, (H, 1)) * u[:, None]).astype(np.float32),
        "w1_words": packed_w1[0],
        "w1_scales": packed_w1[1],
        "w2_words": packed_w2[0],
        "w2_scales": packed_w2[1],
        "offs": striped(np.random.permutation(T)[:S]),
        "k1": striped8(np.random.randint(0, G, (8, H))),
        "two": striped(np.random.permutation(T)[:S]),
        "n1": striped(np.random.permutation(S)),
        "n2": striped(np.random.permutation(S)),
        "n3": striped8(np.stack([np.random.permutation(S) for _ in range(8)])),
        "n4": striped8(np.stack([np.random.permutation(S) for _ in range(8)])),
        "n5": striped8(np.stack([np.random.permutation(S) for _ in range(8)])),
        "n6": striped8(np.stack([np.random.permutation(S) for _ in range(8)])),
        "n7": striped8(np.stack([np.random.permutation(S) for _ in range(8)])),
        "n8": striped8(np.stack([np.random.permutation(S) for _ in range(8)])),
        "n9": striped8(np.stack([np.random.permutation(S) for _ in range(8)])),
    }


def reference(x_words, x_scales, d_words, d_scales, gn, gm, w1_words, w1_scales, w2_words, w2_scales, offs, k1, two, n1, n2, n3, n4, n5, n6, n7, n8, n9):
    d_k1 = unpack_weight(d_words, d_scales)[np.arange(K)[:, None], runs(k1, K)]
    xq = unpack_weight(x_words, x_scales)[:, unstriped(offs)]
    a = 0.0625 * (d_k1.T @ xq)
    z = f64(gn) * ((a - a[:, unstriped(n1)]) * (sigmoid(a[:, unstriped(n2)])))
    x_two = unpack_weight(x_words, x_scales)[:, unstriped(two)]
    b = 0.0625 * (d_k1.T @ x_two)
    ex = np.exp(0.5 * b)
    z2 = f64(gm) * (np.log((ex + ex[np.arange(H)[:, None], runs(n3, H)]) / (ex[np.arange(H)[:, None], runs(n4, H)] + ex[np.arange(H)[:, None], runs(n5, H)])))
    h = unpack_weight(w1_words, w1_scales).T @ mxq(z, 0, "e4m3") + unpack_weight(w2_words, w2_scales).T @ mxq(z2, 0, "e4m3")
    out_0 = 0.75 * ((h[np.arange(N)[:, None], runs(n6, N)]) * (h[np.arange(N)[:, None], runs(n7, N)]) - ((h[np.arange(N)[:, None], runs(n8, N)]) * (h[np.arange(N)[:, None], runs(n9, N)])))
    return (out_0,) + planes(out_0)

@@ -1,0 +1,241 @@
+import math
+from contextlib import ExitStack
+
+import concourse.mybir as mybir
+
+F32 = mybir.dt.float32
+BF16 = mybir.dt.bfloat16
+I32 = mybir.dt.int32
+U32 = mybir.dt.uint32
+U16 = mybir.dt.uint16
+U8 = mybir.dt.uint8
+FP8X4 = mybir.dt.float8_e4m3fn_x4
+ALU = mybir.AluOpType
+ACT = mybir.ActivationFunctionType
+
+P = 128
+PACK = 4
+S = 512
+T = 1024
+G = 2048
+HALF = S // 2
+LIST_COLS = S // 16
+FLOPS = 4 * 2 * 512 * 512 * 512
+
+
+def tile_picked_kjgdifoddsdet_none_po_kernel(
+    tc, x_words, x_scales, d_words, d_scales, gn, gm, w1_words, w1_scales, w2_words, w2_scales,
+    offs, k1, two, n1, n2, n3, n4, n5, n6, n7, n8, n9, out_0, out_1, out_2,
+):
+    nc = tc.nc
+    with ExitStack() as ctx:
+        keep = ctx.enter_context(tc.tile_pool(name="keep", bufs=1))
+        psum = ctx.enter_context(tc.psum_pool(name="psum", bufs=1))
+
+        def sb(name, shape, dtype, tag=None):
+            return keep.tile(shape, dtype, name=name, tag=tag or name, align_bytes=64)
+
+        def load_list(name, src):
+            tile = sb(name, [P, LIST_COLS], U16)
+            nc.sync.dma_start(tile[:], src)
+            return tile
+
+        def load_words(name, src, cols):
+            tile = sb(name, [P, cols], U32)
+            nc.sync.dma_start(tile[:].bitcast(I32), src[0].rearrange("p n t -> p (n t)").bitcast(I32))
+            return tile
+
+        def deal(dst, src):
+            nc.vector.tensor_copy(dst[:].rearrange("p (t m) -> p t m", t=PACK), src[:].rearrange("p (m t) -> p t m", t=PACK))
+
+        def half_of(lst, h):
+            return lst[:, h * LIST_COLS // 2 : (h + 1) * LIST_COLS // 2]
+
+        def cols(h):
+            return slice(h * HALF, (h + 1) * HALF)
+
+        def rows(t):
+            return slice(t * P, (t + 1) * P)
+
+        def weave(dst, src):
+            nc.vector.tensor_copy(
+                dst[:].rearrange("p (c i t) -> p c t i", i=4, t=PACK), src[:].rearrange("p t (c i) -> p c t i", i=4)
+            )
+
+        ds_table = sb("ds_table", [P, G], U8)
+        xs_table = sb("xs_table", [P, T], U8)
+        ds_plane = sb("ds_plane", [P, S], U8)
+        ws_raw = sb("ws_raw", [P, S], U8)
+        nc.gpsimd.memset(ds_table[:].bitcast(I32), 0)
+        nc.vector.memset(xs_table[:].bitcast(I32), 0)
+        nc.gpsimd.memset(ws_raw[:].bitcast(I32), 0)
+        nc.vector.memset(ds_plane[:].bitcast(I32), 0)
+
+        k1_t = load_list("k1_t", k1)
+        nc.scalar.dma_start(ds_table[0:P:8, :].bitcast(I32), d_scales[0].bitcast(I32))
+        two_t = load_list("two_t", two)
+        xw_table = load_words("xw_table", x_words, T)
+        dw_table = load_words("dw_table", d_words, G)
+        for r in range(4):
+            nc.scalar.dma_start(xs_table[r:P:32, :].bitcast(I32), x_scales[0].bitcast(I32)[r:16:4, :])
+        offs_t = load_list("offs_t", offs)
+        for r in range(4):
+            nc.gpsimd.dma_start(ws_raw[4 + r : P : 32, :].bitcast(I32), w2_scales[0].bitcast(I32)[r:16:4, :])
+            nc.gpsimd.dma_start(ws_raw[r:P:32, :].bitcast(I32), w1_scales[0].bitcast(I32)[r:16:4, :])
+
+        ds_picked = sb("ds_picked", [P, S], U8)
+        ds_dealt = sb("ds_dealt", [P, S], U8)
+        nc.vector.tensor_copy(ds_picked[:], ds_table[:].indirect(k1_t[:]))
+        deal(ds_dealt, ds_picked)
+        for r in range(4):
+            nc.scalar.dma_start(ds_plane[r:P:32, :].bitcast(I32), ds_dealt[8 * r : P : 32, :].bitcast(I32))
+
+        n4_t = load_list("n4_t", n4)
+        n5_t = load_list("n5_t", n5)
+        n3_t = load_list("n3_t", n3)
+        w2_raw = load_words("w2_raw", w2_words, S)
+        w1_raw = load_words("w1_raw", w1_words, S)
+        gn_t = sb("gn_t", [P, PACK], F32)
+        nc.sync.dma_start(gn_t[:], gn.rearrange("(p t) o -> p (t o)", t=PACK))
+        gm_t = sb("gm_t", [P, PACK], F32)
+        nc.sync.dma_start(gm_t[:], gm.rearrange("(p t) o -> p (t o)", t=PACK))
+        n1_t = load_list("n1_t", n1)
+        n2_t = load_list("n2_t", n2)
+        n6_t = load_list("n6_t", n6)
+        n7_t = load_list("n7_t", n7)
+        n8_t = load_list("n8_t", n8)
+        n9_t = load_list("n9_t", n9)
+
+        xs_b = sb("xs_b", [P, S], U8)
+        xw_b = sb("xw_b", [P, S], U32)
+        xs_a = sb("xs_a", [P, S], U8)
+        xw_a = sb("xw_a", [P, S], U32)
+        dw_picked = sb("dw_picked", [P, S], U32)
+        dw_dealt = sb("dw_dealt", [P, S], U32)
+        nc.vector.tensor_copy(xw_b[:], xw_table[:].indirect(two_t[:]))
+        nc.vector.tensor_copy(xs_b[:], xs_table[:].indirect(two_t[:]))
+        nc.vector.tensor_copy(dw_picked[:], dw_table[:].indirect(k1_t[:]))
+        deal(dw_dealt, dw_picked)
+        nc.vector.tensor_copy(xw_a[:], xw_table[:].indirect(offs_t[:]))
+        nc.vector.tensor_copy(xs_a[:], xs_table[:].indirect(offs_t[:]))
+
+        def scores(name, words, scales):
+            banks = [psum.tile([P, S], F32, name=f"{name}{t}", tag=f"{name}{t}") for t in range(PACK)]
+            for t in range(PACK):
+                nc.tensor.matmul_mx(
+                    out=banks[t][:], lhsT=dw_dealt[:, rows(t)].bitcast(FP8X4), lhsT_scale=ds_plane[:, rows(t)],
+                    rhs=words[:].bitcast(FP8X4), rhs_scale=scales[:], start=True, stop=True,
+                )
+            return banks
+
+        b_banks = scores("bank_b", xw_b, xs_b)
+        a_banks = scores("bank_a", xw_a, xs_a)
+
+        w1_dealt = sb("w1_dealt", [P, S], U32)
+        w2_dealt = sb("w2_dealt", [P, S], U32)
+        ws_dealt = sb("ws_dealt", [P, S], U8)
+        deal(w2_dealt, w2_raw)
+        deal(w1_dealt, w1_raw)
+        deal(ws_dealt, ws_raw)
+        neg_gn = sb("neg_gn", [P, PACK], F32)
+        nc.vector.tensor_scalar(neg_gn[:], gn_t[:], -1.0, None, ALU.mult)
+
+        ex = [sb(f"ex{t}", [P, S], F32) for t in range(PACK)]
+        ex_copy = [sb(f"ex_copy{t}", [P, S], F32) for t in range(PACK)]
+        a_sb = [sb(f"a_sb{t}", [P, S], F32) for t in range(PACK)]
+        a_copy = [sb(f"a_copy{t}", [P, S], F32) for t in range(PACK)]
+        ex4 = [sb(f"ex4_{t}", [P, S], F32) for t in range(PACK)]
+        sums = [sb(f"sums{t}", [P, 2 * S], F32) for t in range(PACK)]
+        logs = [sb(f"logs{t}", [P, 2 * S], F32) for t in range(PACK)]
+        den_g = [sb(f"den_g{t}", [P, S], F32) for t in range(PACK)]
+        diff = [sb(f"diff{t}", [P, S], F32) for t in range(PACK)]
+        for t in range(PACK):
+            nc.scalar.activation(ex[t][:], b_banks[t][:], ACT.Exp, scale=0.5 * 0.0625)
+            nc.sync.dma_start(ex_copy[t][:], ex[t][:])
+        for t in range(PACK):
+            for h in range(2):
+                nc.scalar.activation(ex4[t][:, cols(h)], ex[t][:].indirect(half_of(n4_t, h)), ACT.Copy)
+            for h in range(2):
+                nc.vector.tensor_tensor(
+                    sums[t][:, S + h * HALF : S + (h + 1) * HALF], ex[t][:].indirect(half_of(n5_t, h)), ex4[t][:, cols(h)], ALU.add
+                )
+            for h in range(2):
+                nc.vector.tensor_tensor(sums[t][:, cols(h)], ex[t][:].indirect(half_of(n3_t, h)), ex_copy[t][:, cols(h)], ALU.add)
+        for t in range(PACK):
+            nc.scalar.activation(a_sb[t][:], a_banks[t][:], ACT.Copy, scale=0.0625)
+            nc.sync.dma_start(a_copy[t][:], a_sb[t][:])
+        for t in range(PACK):
+            nc.scalar.activation(logs[t][:], sums[t][:], ACT.Ln)
+            nc.scalar.activation(den_g[t][:], logs[t][:, S:], ACT.Copy, scale=gm_t[:, t : t + 1])
+        for t in range(PACK):
+            for h in range(2):
+                nc.vector.tensor_tensor(diff[t][:, cols(h)], a_sb[t][:].indirect(half_of(n1_t, h)), a_copy[t][:, cols(h)], ALU.subtract)
+
+        z2 = sb("z2", [P, PACK, S], F32)
+        for t in range(PACK):
+            nc.vector.scalar_tensor_tensor(z2[:, t, :], logs[t][:, :S], gm_t[:, t : t + 1], den_g[t][:], ALU.mult, ALU.subtract)
+        z2_bf = sb("z2_bf", [P, PACK * S], BF16)
+        z2_w = sb("z2_w", [P, S], U32)
+        z2_s = sb("z2_s", [P, S], U8)
+        weave(z2_bf, z2)
+        nc.vector.quantize_mx(out=z2_w[:].bitcast(FP8X4), scales=z2_s[:], in_=z2_bf[:])
+
+        h_banks = [
+            [psum.tile([P, HALF], F32, name=f"h{h}{t}", tag=f"{('bank_b', 'bank_a')[h]}{t}") for t in range(PACK)] for h in range(2)
+        ]
+        for h in range(2):
+            for t in range(PACK):
+                nc.tensor.matmul_mx(
+                    out=h_banks[h][t][:], lhsT=w2_dealt[:, rows(t)].bitcast(FP8X4), lhsT_scale=ws_dealt[4:P, rows(t)],
+                    rhs=z2_w[:, cols(h)].bitcast(FP8X4), rhs_scale=z2_s[:, cols(h)], start=True, stop=False,
+                )
+
+        hs = [sb(f"hs{t}", [P, S], F32) for t in range(PACK)]
+        root = math.sqrt(0.75)
+        for h in range(2):
+            sig = sb(f"sig{h}", [P, PACK, HALF], F32, tag=f"sums{PACK - 1 - h}")
+            z = sb(f"z{h}", [P, PACK, HALF], F32)
+            for t in range(PACK):
+                nc.scalar.activation(sig[:, t, :], a_sb[t][:].indirect(half_of(n2_t, h)), ACT.Sigmoid)
+                nc.vector.scalar_tensor_tensor(z[:, t, :], diff[t][:, cols(h)], neg_gn[:, t : t + 1], sig[:, t, :], ALU.mult, ALU.mult)
+            z_bf = sb(f"z_bf{h}", [P, PACK * HALF], BF16)
+            z_w = sb(f"z_w{h}", [P, HALF], U32)
+            z_s = sb(f"z_s{h}", [P, HALF], U8)
+            weave(z_bf, z)
+            nc.vector.quantize_mx(out=z_w[:].bitcast(FP8X4), scales=z_s[:], in_=z_bf[:])
+            for t in range(PACK):
+                nc.tensor.matmul_mx(
+                    out=h_banks[h][t][:], lhsT=w1_dealt[:, rows(t)].bitcast(FP8X4), lhsT_scale=ws_dealt[:, rows(t)],
+                    rhs=z_w[:].bitcast(FP8X4), rhs_scale=z_s[:], start=False, stop=True,
+                )
+        for h in range(2):
+            for t in range(PACK):
+                nc.scalar.activation(hs[t][:, cols(h)], h_banks[h][t][:], ACT.Copy, scale=root)
+
+        out_rows = out_0.rearrange("(p t) j -> p t j", t=PACK)
+        out_words = out_1[0].rearrange("p n t -> p (n t)").bitcast(I32)
+        out_scales = out_2[0].bitcast(I32)
+        o_s = sb("o_s", [P, S], U8)
+        for h in range(2):
+            h6 = sb(f"h6_{h}", [P, PACK, HALF], F32)
+            h8 = sb(f"h8_{h}", [P, PACK, HALF], F32)
+            p67 = sb(f"p67_{h}", [P, PACK, HALF], F32)
+            p89 = sb(f"p89_{h}", [P, PACK, HALF], F32)
+            res = sb(f"res{h}", [P, PACK, HALF], F32)
+            for t in range(PACK + 1):
+                if t < PACK:
+                    nc.scalar.activation(h6[:, t, :], hs[t][:].indirect(half_of(n6_t, h)), ACT.Copy)
+                    nc.scalar.activation(h8[:, t, :], hs[t][:].indirect(half_of(n8_t, h)), ACT.Copy)
+                    nc.vector.tensor_tensor(p67[:, t, :], hs[t][:].indirect(half_of(n7_t, h)), h6[:, t, :], ALU.mult)
+                    nc.vector.tensor_tensor(p89[:, t, :], hs[t][:].indirect(half_of(n9_t, h)), h8[:, t, :], ALU.mult)
+                if t > 0:
+                    nc.vector.tensor_tensor(res[:, t - 1, :], p67[:, t - 1, :], p89[:, t - 1, :], ALU.subtract)
+                    nc.sync.dma_start(out_rows[:, t - 1, cols(h)], res[:, t - 1, :])
+            o_bf = sb(f"o_bf{h}", [P, PACK * HALF], BF16)
+            o_w = sb(f"o_w{h}", [P, HALF], U32)
+            weave(o_bf, res)
+            nc.vector.quantize_mx(out=o_w[:].bitcast(FP8X4), scales=o_s[:, cols(h)], in_=o_bf[:])
+            nc.sync.dma_start(out_words[:, cols(h)], o_w[:].bitcast(I32))
+        for r in range(4):
+            queue = nc.scalar if r % 2 else nc.sync
+            queue.dma_start(out_scales[r:16:4, :], o_s[r:P:32, :].bitcast(I32))

@@ -19,6 +19,7 @@ S = 512
 T = 1024
 G = 2048
 HALF = S // 2
+QUARTER = S // 4
 LIST_COLS = S // 16
 FLOPS = 4 * 2 * 512 * 512 * 512
 
@@ -40,16 +41,16 @@ def tile_picked_kjgdifoddsdet_none_po_kernel(
             nc.sync.dma_start(tile[:], src)
             return tile
 
-        def load_words(name, src, cols):
-            tile = sb(name, [P, cols], U32)
+        def load_words(name, src, cols, tag=None):
+            tile = sb(name, [P, cols], U32, tag)
             nc.sync.dma_start(tile[:].bitcast(I32), src[0].rearrange("p n t -> p (n t)").bitcast(I32))
             return tile
 
         def deal(dst, src):
             nc.vector.tensor_copy(dst[:].rearrange("p (t m) -> p t m", t=PACK), src[:].rearrange("p (m t) -> p t m", t=PACK))
 
-        def half_of(lst, h):
-            return lst[:, h * LIST_COLS // 2 : (h + 1) * LIST_COLS // 2]
+        def part(lst, lo, hi):
+            return lst[:, lo // 16 : hi // 16]
 
         def cols(h):
             return slice(h * HALF, (h + 1) * HALF)
@@ -57,48 +58,35 @@ def tile_picked_kjgdifoddsdet_none_po_kernel(
         def rows(t):
             return slice(t * P, (t + 1) * P)
 
-        def weave(dst, src):
-            nc.vector.tensor_copy(
+        def weave(dst, src, copy=nc.vector.tensor_copy):
+            copy(
                 dst[:].rearrange("p (c i t) -> p c t i", i=4, t=PACK), src[:].rearrange("p t (c i) -> p c t i", i=4)
             )
 
         ds_table = sb("ds_table", [P, G], U8)
         xs_table = sb("xs_table", [P, T], U8)
-        ds_plane = sb("ds_plane", [P, S], U8)
-        ws_raw = sb("ws_raw", [P, S], U8)
-        nc.gpsimd.memset(ds_table[:].bitcast(I32), 0)
+        planes_b = sb("planes_b", [P, 2 * S], U8)
+        plane_a = sb("plane_a", [P, S], U8)
+        nc.vector.memset(ds_table[:, : G // 2].bitcast(I32), 0)
+        nc.gpsimd.memset(ds_table[:, G // 2 :].bitcast(I32), 0)
         nc.vector.memset(xs_table[:].bitcast(I32), 0)
-        nc.gpsimd.memset(ws_raw[:].bitcast(I32), 0)
-        nc.vector.memset(ds_plane[:].bitcast(I32), 0)
+        nc.gpsimd.memset(planes_b[:].bitcast(I32), 0)
+        nc.gpsimd.memset(plane_a[:].bitcast(I32), 0)
+        ex = [sb(f"ex{t}", [P, 2 * S], F32) for t in range(PACK)]
+        a_sb = [sb(f"a_sb{t}", [P, 2 * S], F32) for t in range(PACK)]
+        for window in ex + a_sb:
+            nc.gpsimd.memset(window[:, S:], 0.0)
 
         k1_t = load_list("k1_t", k1)
-        nc.scalar.dma_start(ds_table[0:P:8, :].bitcast(I32), d_scales[0].bitcast(I32))
+        nc.sync.dma_start(ds_table[0:P:8, :].bitcast(I32), d_scales[0].bitcast(I32))
         two_t = load_list("two_t", two)
+        nc.sync.dma_start(xs_table[0:P:8, :].bitcast(I32), x_scales[0].bitcast(I32))
+        offs_t = load_list("offs_t", offs)
+        n4_t = load_list("n4_t", n4)
         xw_table = load_words("xw_table", x_words, T)
         dw_table = load_words("dw_table", d_words, G)
-        for r in range(4):
-            nc.scalar.dma_start(xs_table[r:P:32, :].bitcast(I32), x_scales[0].bitcast(I32)[r:16:4, :])
-        offs_t = load_list("offs_t", offs)
-        for r in range(4):
-            nc.gpsimd.dma_start(ws_raw[4 + r : P : 32, :].bitcast(I32), w2_scales[0].bitcast(I32)[r:16:4, :])
-            nc.gpsimd.dma_start(ws_raw[r:P:32, :].bitcast(I32), w1_scales[0].bitcast(I32)[r:16:4, :])
-
-        ds_picked = sb("ds_picked", [P, S], U8)
-        ds_dealt = sb("ds_dealt", [P, S], U8)
-        nc.vector.tensor_copy(ds_picked[:], ds_table[:].indirect(k1_t[:]))
-        deal(ds_dealt, ds_picked)
-        for r in range(4):
-            nc.scalar.dma_start(ds_plane[r:P:32, :].bitcast(I32), ds_dealt[8 * r : P : 32, :].bitcast(I32))
-
-        n4_t = load_list("n4_t", n4)
         n5_t = load_list("n5_t", n5)
         n3_t = load_list("n3_t", n3)
-        w2_raw = load_words("w2_raw", w2_words, S)
-        w1_raw = load_words("w1_raw", w1_words, S)
-        gn_t = sb("gn_t", [P, PACK], F32)
-        nc.sync.dma_start(gn_t[:], gn.rearrange("(p t) o -> p (t o)", t=PACK))
-        gm_t = sb("gm_t", [P, PACK], F32)
-        nc.sync.dma_start(gm_t[:], gm.rearrange("(p t) o -> p (t o)", t=PACK))
         n1_t = load_list("n1_t", n1)
         n2_t = load_list("n2_t", n2)
         n6_t = load_list("n6_t", n6)
@@ -106,43 +94,60 @@ def tile_picked_kjgdifoddsdet_none_po_kernel(
         n8_t = load_list("n8_t", n8)
         n9_t = load_list("n9_t", n9)
 
+        def place_rows(queue, plane, src):
+            for r in range(4):
+                queue.dma_start(plane[r:P:32, :].bitcast(I32), src[8 * r : P : 32, :].bitcast(I32))
+
+        ds_picked = sb("ds_picked", [P, S], U8)
         xs_b = sb("xs_b", [P, S], U8)
+        rows_b = sb("rows_b", [P, 2 * S], U8)
         xw_b = sb("xw_b", [P, S], U32)
-        xs_a = sb("xs_a", [P, S], U8)
-        xw_a = sb("xw_a", [P, S], U32)
         dw_picked = sb("dw_picked", [P, S], U32)
         dw_dealt = sb("dw_dealt", [P, S], U32)
-        nc.vector.tensor_copy(xw_b[:], xw_table[:].indirect(two_t[:]))
+        nc.vector.tensor_copy(ds_picked[:], ds_table[:].indirect(k1_t[:]))
         nc.vector.tensor_copy(xs_b[:], xs_table[:].indirect(two_t[:]))
+        deal(rows_b[:, :S], ds_picked)
+        nc.vector.tensor_copy(rows_b[:, S:].bitcast(I32), xs_b[:].bitcast(I32))
+        place_rows(nc.scalar, planes_b, rows_b)
+        nc.vector.tensor_copy(xw_b[:], xw_table[:].indirect(two_t[:]))
         nc.vector.tensor_copy(dw_picked[:], dw_table[:].indirect(k1_t[:]))
         deal(dw_dealt, dw_picked)
-        nc.vector.tensor_copy(xw_a[:], xw_table[:].indirect(offs_t[:]))
+        xs_a = sb("xs_a", [P, S], U8, "dw_table")
+        xw_a = sb("xw_a", [P, S], U32, "dw_picked")
         nc.vector.tensor_copy(xs_a[:], xs_table[:].indirect(offs_t[:]))
+        place_rows(nc.sync, plane_a, xs_a)
+        nc.vector.tensor_copy(xw_a[:], xw_table[:].indirect(offs_t[:]))
+        gn_t = sb("gn_t", [P, PACK], F32, "ds_picked")
+        nc.gpsimd.dma_start(gn_t[:], gn.rearrange("(p t) o -> p (t o)", t=PACK))
+        gm_t = sb("gm_t", [P, PACK], F32, "xs_b")
+        nc.gpsimd.dma_start(gm_t[:], gm.rearrange("(p t) o -> p (t o)", t=PACK))
 
         def scores(name, words, scales):
             banks = [psum.tile([P, S], F32, name=f"{name}{t}", tag=f"{name}{t}") for t in range(PACK)]
             for t in range(PACK):
                 nc.tensor.matmul_mx(
-                    out=banks[t][:], lhsT=dw_dealt[:, rows(t)].bitcast(FP8X4), lhsT_scale=ds_plane[:, rows(t)],
-                    rhs=words[:].bitcast(FP8X4), rhs_scale=scales[:], start=True, stop=True,
+                    out=banks[t][:], lhsT=dw_dealt[:, rows(t)].bitcast(FP8X4), lhsT_scale=planes_b[:, rows(t)],
+                    rhs=words[:].bitcast(FP8X4), rhs_scale=scales, start=True, stop=True,
                 )
             return banks
 
-        b_banks = scores("bank_b", xw_b, xs_b)
-        a_banks = scores("bank_a", xw_a, xs_a)
+        b_banks = scores("bank_b", xw_b, planes_b[:, S:])
+        a_banks = scores("bank_a", xw_a, plane_a[:])
 
+        ws_raw = sb("ws_raw", [P, S], U8, "rows_b")
+        nc.gpsimd.memset(ws_raw[:].bitcast(I32), 0)
+        w2_raw = load_words("w2_raw", w2_words, S, "xw_table")
+        w1_raw = load_words("w1_raw", w1_words, S, "xw_b")
+        for r in range(4):
+            nc.sync.dma_start(ws_raw[4 + r : P : 32, :].bitcast(I32), w2_scales[0].bitcast(I32)[r:16:4, :])
+            nc.sync.dma_start(ws_raw[r:P:32, :].bitcast(I32), w1_scales[0].bitcast(I32)[r:16:4, :])
         w1_dealt = sb("w1_dealt", [P, S], U32)
         w2_dealt = sb("w2_dealt", [P, S], U32)
         ws_dealt = sb("ws_dealt", [P, S], U8)
-        deal(w2_dealt, w2_raw)
-        deal(w1_dealt, w1_raw)
-        deal(ws_dealt, ws_raw)
         neg_gn = sb("neg_gn", [P, PACK], F32)
-        nc.vector.tensor_scalar(neg_gn[:], gn_t[:], -1.0, None, ALU.mult)
+        nc.gpsimd.tensor_scalar(neg_gn[:], gn_t[:], -1.0, 0.0, ALU.mult, ALU.add)
 
-        ex = [sb(f"ex{t}", [P, S], F32) for t in range(PACK)]
         ex_copy = [sb(f"ex_copy{t}", [P, S], F32) for t in range(PACK)]
-        a_sb = [sb(f"a_sb{t}", [P, S], F32) for t in range(PACK)]
         a_copy = [sb(f"a_copy{t}", [P, S], F32) for t in range(PACK)]
         ex4 = [sb(f"ex4_{t}", [P, S], F32) for t in range(PACK)]
         sums = [sb(f"sums{t}", [P, 2 * S], F32) for t in range(PACK)]
@@ -150,27 +155,25 @@ def tile_picked_kjgdifoddsdet_none_po_kernel(
         den_g = [sb(f"den_g{t}", [P, S], F32) for t in range(PACK)]
         diff = [sb(f"diff{t}", [P, S], F32) for t in range(PACK)]
         for t in range(PACK):
-            nc.scalar.activation(ex[t][:], b_banks[t][:], ACT.Exp, scale=0.5 * 0.0625)
-            nc.sync.dma_start(ex_copy[t][:], ex[t][:])
+            if t < 2:
+                for u in (2 * t, 2 * t + 1):
+                    nc.scalar.activation(ex[u][:, :S], b_banks[u][:], ACT.Exp, scale=0.5 * 0.0625)
+                    nc.sync.dma_start(ex_copy[u][:], ex[u][:, :S])
+            nc.scalar.activation(ex4[t][:], ex[t][:].indirect(n4_t[:]), ACT.Copy)
+            nc.vector.tensor_tensor(sums[t][:, S:], ex[t][:].indirect(n5_t[:]), ex4[t][:], ALU.add)
+            nc.vector.tensor_tensor(sums[t][:, :S], ex[t][:].indirect(n3_t[:]), ex_copy[t][:], ALU.add)
         for t in range(PACK):
-            for h in range(2):
-                nc.scalar.activation(ex4[t][:, cols(h)], ex[t][:].indirect(half_of(n4_t, h)), ACT.Copy)
-            for h in range(2):
-                nc.vector.tensor_tensor(
-                    sums[t][:, S + h * HALF : S + (h + 1) * HALF], ex[t][:].indirect(half_of(n5_t, h)), ex4[t][:, cols(h)], ALU.add
-                )
-            for h in range(2):
-                nc.vector.tensor_tensor(sums[t][:, cols(h)], ex[t][:].indirect(half_of(n3_t, h)), ex_copy[t][:, cols(h)], ALU.add)
-        for t in range(PACK):
-            nc.scalar.activation(a_sb[t][:], a_banks[t][:], ACT.Copy, scale=0.0625)
-            nc.sync.dma_start(a_copy[t][:], a_sb[t][:])
+            nc.scalar.activation(a_sb[t][:, :S], a_banks[t][:], ACT.Copy, scale=0.0625)
+            nc.sync.dma_start(a_copy[t][:], a_sb[t][:, :S])
         for t in range(PACK):
             nc.scalar.activation(logs[t][:], sums[t][:], ACT.Ln)
             nc.scalar.activation(den_g[t][:], logs[t][:, S:], ACT.Copy, scale=gm_t[:, t : t + 1])
         for t in range(PACK):
-            for h in range(2):
-                nc.vector.tensor_tensor(diff[t][:, cols(h)], a_sb[t][:].indirect(half_of(n1_t, h)), a_copy[t][:, cols(h)], ALU.subtract)
+            nc.vector.tensor_tensor(diff[t][:], a_sb[t][:].indirect(n1_t[:]), a_copy[t][:], ALU.subtract)
 
+        deal(w2_dealt, w2_raw)
+        deal(w1_dealt, w1_raw)
+        deal(ws_dealt, ws_raw)
         z2 = sb("z2", [P, PACK, S], F32)
         for t in range(PACK):
             nc.vector.scalar_tensor_tensor(z2[:, t, :], logs[t][:, :S], gm_t[:, t : t + 1], den_g[t][:], ALU.mult, ALU.subtract)
@@ -190,50 +193,71 @@ def tile_picked_kjgdifoddsdet_none_po_kernel(
                     rhs=z2_w[:, cols(h)].bitcast(FP8X4), rhs_scale=z2_s[:, cols(h)], start=True, stop=False,
                 )
 
-        hs = [sb(f"hs{t}", [P, S], F32) for t in range(PACK)]
+        hs = [sb(f"hs{t}", [P, 2 * S], F32) for t in range(PACK)]
+        for window in hs:
+            nc.gpsimd.memset(window[:, S:], 0.0)
         root = math.sqrt(0.75)
-        for h in range(2):
-            sig = sb(f"sig{h}", [P, PACK, HALF], F32, tag=f"sums{PACK - 1 - h}")
-            z = sb(f"z{h}", [P, PACK, HALF], F32)
+        sig = sb("sig", [P, PACK, S], F32, f"sums{PACK - 1}")
+        for k, (lo, hi) in enumerate(((0, HALF), (HALF, HALF + QUARTER), (HALF + QUARTER, S))):
+            h, width = lo // HALF, hi - lo
+            z = sb(f"z{k}", [P, PACK, width], F32)
             for t in range(PACK):
-                nc.scalar.activation(sig[:, t, :], a_sb[t][:].indirect(half_of(n2_t, h)), ACT.Sigmoid)
-                nc.vector.scalar_tensor_tensor(z[:, t, :], diff[t][:, cols(h)], neg_gn[:, t : t + 1], sig[:, t, :], ALU.mult, ALU.mult)
-            z_bf = sb(f"z_bf{h}", [P, PACK * HALF], BF16)
-            z_w = sb(f"z_w{h}", [P, HALF], U32)
-            z_s = sb(f"z_s{h}", [P, HALF], U8)
+                nc.scalar.activation(sig[:, t, lo:hi], a_sb[t][:].indirect(part(n2_t, lo, hi)), ACT.Sigmoid)
+                nc.vector.scalar_tensor_tensor(z[:, t, :], diff[t][:, lo:hi], neg_gn[:, t : t + 1], sig[:, t, lo:hi], ALU.mult, ALU.mult)
+            z_bf = sb(f"z_bf{k}", [P, PACK * width], BF16)
+            z_w = sb(f"z_w{k}", [P, width], U32)
+            z_s = sb(f"z_s{k}", [P, width], U8)
             weave(z_bf, z)
             nc.vector.quantize_mx(out=z_w[:].bitcast(FP8X4), scales=z_s[:], in_=z_bf[:])
             for t in range(PACK):
                 nc.tensor.matmul_mx(
-                    out=h_banks[h][t][:], lhsT=w1_dealt[:, rows(t)].bitcast(FP8X4), lhsT_scale=ws_dealt[:, rows(t)],
-                    rhs=z_w[:].bitcast(FP8X4), rhs_scale=z_s[:], start=False, stop=True,
+                    out=h_banks[h][t][:, lo - h * HALF : hi - h * HALF], lhsT=w1_dealt[:, rows(t)].bitcast(FP8X4),
+                    lhsT_scale=ws_dealt[:, rows(t)], rhs=z_w[:].bitcast(FP8X4), rhs_scale=z_s[:],
+                    start=False, stop=(hi % HALF == 0),
                 )
         for h in range(2):
             for t in range(PACK):
-                nc.scalar.activation(hs[t][:, cols(h)], h_banks[h][t][:], ACT.Copy, scale=root)
+                if h == 1 and t > 0:
+                    nc.vector.tensor_scalar(hs[t][:, cols(h)], h_banks[h][t][:], root, None, ALU.mult)
+                else:
+                    nc.scalar.activation(hs[t][:, cols(h)], h_banks[h][t][:], ACT.Copy, scale=root)
 
         out_rows = out_0.rearrange("(p t) j -> p t j", t=PACK)
         out_words = out_1[0].rearrange("p n t -> p (n t)").bitcast(I32)
         out_scales = out_2[0].bitcast(I32)
         o_s = sb("o_s", [P, S], U8)
+        res = [sb(f"res{h}", [P, PACK, HALF], F32) for h in range(2)]
+        steps = [(0, 0, HALF), (0, HALF, S), (1, 0, S), (2, 0, S), (3, 0, HALF), (3, HALF, S)]
+        h6 = [sb(f"h6_{t}", [P, S], F32, f"ex4_{t}") for t in range(PACK)]
+        h8 = [sb(f"h8_{t}", [P, S], F32, f"ex_copy{t}") for t in range(PACK)]
+        h9 = sb("h9", [P, S], F32)
+        p67 = [sb(f"p67_{t}", [P, S], F32, f"a_copy{t}") for t in range(PACK)]
+        p89 = [sb(f"p89_{t}", [P, S], F32, f"den_g{t}") for t in range(PACK)]
+
+        def products(t, lo, hi):
+            nc.scalar.activation(h6[t][:, lo:hi], hs[t][:].indirect(part(n6_t, lo, hi)), ACT.Copy)
+            nc.scalar.activation(h8[t][:, lo:hi], hs[t][:].indirect(part(n8_t, lo, hi)), ACT.Copy)
+            nc.vector.tensor_tensor(p67[t][:, lo:hi], hs[t][:].indirect(part(n7_t, lo, hi)), h6[t][:, lo:hi], ALU.mult)
+            if t == PACK - 1:
+                nc.scalar.activation(h9[:, lo:hi], hs[t][:].indirect(part(n9_t, lo, hi)), ACT.Copy)
+                nc.vector.tensor_tensor(p89[t][:, lo:hi], h9[:, lo:hi], h8[t][:, lo:hi], ALU.mult)
+            else:
+                nc.vector.tensor_tensor(p89[t][:, lo:hi], hs[t][:].indirect(part(n9_t, lo, hi)), h8[t][:, lo:hi], ALU.mult)
+
+        def finish(t, lo, hi):
+            for h in range(lo // HALF, hi // HALF):
+                nc.vector.tensor_tensor(res[h][:, t, :], p67[t][:, cols(h)], p89[t][:, cols(h)], ALU.subtract)
+                nc.sync.dma_start(out_rows[:, t, cols(h)], res[h][:, t, :])
+
+        for k in range(len(steps) + 1):
+            if k < len(steps):
+                products(*steps[k])
+            if k > 0:
+                finish(*steps[k - 1])
         for h in range(2):
-            h6 = sb(f"h6_{h}", [P, PACK, HALF], F32)
-            h8 = sb(f"h8_{h}", [P, PACK, HALF], F32)
-            p67 = sb(f"p67_{h}", [P, PACK, HALF], F32)
-            p89 = sb(f"p89_{h}", [P, PACK, HALF], F32)
-            res = sb(f"res{h}", [P, PACK, HALF], F32)
-            for t in range(PACK + 1):
-                if t < PACK:
-                    nc.scalar.activation(h6[:, t, :], hs[t][:].indirect(half_of(n6_t, h)), ACT.Copy)
-                    nc.scalar.activation(h8[:, t, :], hs[t][:].indirect(half_of(n8_t, h)), ACT.Copy)
-                    nc.vector.tensor_tensor(p67[:, t, :], hs[t][:].indirect(half_of(n7_t, h)), h6[:, t, :], ALU.mult)
-                    nc.vector.tensor_tensor(p89[:, t, :], hs[t][:].indirect(half_of(n9_t, h)), h8[:, t, :], ALU.mult)
-                if t > 0:
-                    nc.vector.tensor_tensor(res[:, t - 1, :], p67[:, t - 1, :], p89[:, t - 1, :], ALU.subtract)
-                    nc.sync.dma_start(out_rows[:, t - 1, cols(h)], res[:, t - 1, :])
             o_bf = sb(f"o_bf{h}", [P, PACK * HALF], BF16)
             o_w = sb(f"o_w{h}", [P, HALF], U32)
-            weave(o_bf, res)
+            weave(o_bf, res[h], nc.vector.tensor_copy if h else nc.scalar.copy)
             nc.vector.quantize_mx(out=o_w[:].bitcast(FP8X4), scales=o_s[:, cols(h)], in_=o_bf[:])
             nc.sync.dma_start(out_words[:, cols(h)], o_w[:].bitcast(I32))
         for r in range(4):

@@ -21,6 +21,8 @@ G = 2048
 HALF = S // 2
 QUARTER = S // 4
 LIST_COLS = S // 16
+FUSED_A = 3
+FUSED_C = 3
 FLOPS = 4 * 2 * 512 * 512 * 512
 
 
@@ -74,8 +76,8 @@ def tile_picked_kjgdifoddsdet_none_po_kernel(
         nc.gpsimd.memset(plane_a[:].bitcast(I32), 0)
         ex = [sb(f"ex{t}", [P, 2 * S], F32) for t in range(PACK)]
         a_sb = [sb(f"a_sb{t}", [P, 2 * S], F32) for t in range(PACK)]
-        for window in ex + a_sb:
-            nc.gpsimd.memset(window[:, S:], 0.0)
+        for window in ex:
+            nc.vector.memset(window[:, S:], 0.0)
 
         k1_t = load_list("k1_t", k1)
         nc.sync.dma_start(ds_table[0:P:8, :].bitcast(I32), d_scales[0].bitcast(I32))
@@ -117,10 +119,6 @@ def tile_picked_kjgdifoddsdet_none_po_kernel(
         nc.vector.tensor_copy(xs_a[:], xs_table[:].indirect(offs_t[:]))
         place_rows(nc.sync, plane_a, xs_a)
         nc.vector.tensor_copy(xw_a[:], xw_table[:].indirect(offs_t[:]))
-        gn_t = sb("gn_t", [P, PACK], F32, "ds_picked")
-        nc.gpsimd.dma_start(gn_t[:], gn.rearrange("(p t) o -> p (t o)", t=PACK))
-        gm_t = sb("gm_t", [P, PACK], F32, "xs_b")
-        nc.gpsimd.dma_start(gm_t[:], gm.rearrange("(p t) o -> p (t o)", t=PACK))
 
         def scores(name, words, scales):
             banks = [psum.tile([P, S], F32, name=f"{name}{t}", tag=f"{name}{t}") for t in range(PACK)]
@@ -134,20 +132,7 @@ def tile_picked_kjgdifoddsdet_none_po_kernel(
         b_banks = scores("bank_b", xw_b, planes_b[:, S:])
         a_banks = scores("bank_a", xw_a, plane_a[:])
 
-        ws_raw = sb("ws_raw", [P, S], U8, "rows_b")
-        nc.gpsimd.memset(ws_raw[:].bitcast(I32), 0)
-        w2_raw = load_words("w2_raw", w2_words, S, "xw_table")
-        w1_raw = load_words("w1_raw", w1_words, S, "xw_b")
-        for r in range(4):
-            nc.sync.dma_start(ws_raw[4 + r : P : 32, :].bitcast(I32), w2_scales[0].bitcast(I32)[r:16:4, :])
-            nc.sync.dma_start(ws_raw[r:P:32, :].bitcast(I32), w1_scales[0].bitcast(I32)[r:16:4, :])
-        w1_dealt = sb("w1_dealt", [P, S], U32)
-        w2_dealt = sb("w2_dealt", [P, S], U32)
-        ws_dealt = sb("ws_dealt", [P, S], U8)
-        neg_gn = sb("neg_gn", [P, PACK], F32)
-        nc.gpsimd.tensor_scalar(neg_gn[:], gn_t[:], -1.0, 0.0, ALU.mult, ALU.add)
-
-        ex_copy = [sb(f"ex_copy{t}", [P, S], F32) for t in range(PACK)]
+        ex_copy = [a_sb[t][:, S:] for t in range(PACK)]
         a_copy = [sb(f"a_copy{t}", [P, S], F32) for t in range(PACK)]
         ex4 = [sb(f"ex4_{t}", [P, S], F32) for t in range(PACK)]
         sums = [sb(f"sums{t}", [P, 2 * S], F32) for t in range(PACK)]
@@ -155,22 +140,46 @@ def tile_picked_kjgdifoddsdet_none_po_kernel(
         den_g = [sb(f"den_g{t}", [P, S], F32) for t in range(PACK)]
         diff = [sb(f"diff{t}", [P, S], F32) for t in range(PACK)]
         for t in range(PACK):
-            if t < 2:
-                for u in (2 * t, 2 * t + 1):
-                    nc.scalar.activation(ex[u][:, :S], b_banks[u][:], ACT.Exp, scale=0.5 * 0.0625)
-                    nc.sync.dma_start(ex_copy[u][:], ex[u][:, :S])
-            nc.scalar.activation(ex4[t][:], ex[t][:].indirect(n4_t[:]), ACT.Copy)
+            nc.scalar.activation(ex[t][:, :S], b_banks[t][:], ACT.Exp, scale=0.5 * 0.0625)
+            nc.sync.dma_start(ex_copy[t], ex[t][:, :S])
+        for t in range(PACK):
+            if t == 0:
+                nc.vector.tensor_copy(ex4[t][:], ex[t][:].indirect(n4_t[:]))
+            else:
+                nc.scalar.activation(ex4[t][:], ex[t][:].indirect(n4_t[:]), ACT.Copy)
             nc.vector.tensor_tensor(sums[t][:, S:], ex[t][:].indirect(n5_t[:]), ex4[t][:], ALU.add)
-            nc.vector.tensor_tensor(sums[t][:, :S], ex[t][:].indirect(n3_t[:]), ex_copy[t][:], ALU.add)
+            nc.vector.tensor_tensor(sums[t][:, :S], ex[t][:].indirect(n3_t[:]), ex_copy[t], ALU.add)
+        gm_t = sb("gm_t", [P, PACK], F32, "xw_b")
+        nc.sync.dma_start(gm_t[:], gm.rearrange("(p t) o -> p (t o)", t=PACK))
+        gn_t = sb("gn_t", [P, PACK], F32, "xw_table")
+        nc.sync.dma_start(gn_t[:], gn.rearrange("(p t) o -> p (t o)", t=PACK))
+        ws_raw = sb("ws_raw", [P, S], U8, "dw_table")
+        nc.vector.memset(ws_raw[:].bitcast(I32), 0)
+        w2_raw = load_words("w2_raw", w2_words, S, "ex4_0")
+        w1_raw = load_words("w1_raw", w1_words, S, "dw_picked")
+        for r in range(4):
+            nc.sync.dma_start(ws_raw[4 + r : P : 32, :].bitcast(I32), w2_scales[0].bitcast(I32)[r:16:4, :])
+            nc.sync.dma_start(ws_raw[r:P:32, :].bitcast(I32), w1_scales[0].bitcast(I32)[r:16:4, :])
+        w1_dealt = sb("w1_dealt", [P, S], U32)
+        w2_dealt = sb("w2_dealt", [P, S], U32)
+        ws_dealt = sb("ws_dealt", [P, S], U8)
+        neg_gn = sb("neg_gn", [P, PACK], F32)
         for t in range(PACK):
             nc.scalar.activation(a_sb[t][:, :S], a_banks[t][:], ACT.Copy, scale=0.0625)
-            nc.sync.dma_start(a_copy[t][:], a_sb[t][:, :S])
+            if t < FUSED_A:
+                nc.sync.dma_start(a_copy[t][:], a_sb[t][:, :S])
+        for t in range(FUSED_A, PACK):
+            nc.scalar.activation(a_copy[t][:], a_sb[t][:].indirect(n1_t[:]), ACT.Copy)
         for t in range(PACK):
             nc.scalar.activation(logs[t][:], sums[t][:], ACT.Ln)
             nc.scalar.activation(den_g[t][:], logs[t][:, S:], ACT.Copy, scale=gm_t[:, t : t + 1])
         for t in range(PACK):
-            nc.vector.tensor_tensor(diff[t][:], a_sb[t][:].indirect(n1_t[:]), a_copy[t][:], ALU.subtract)
+            if t < FUSED_A:
+                nc.vector.tensor_tensor(diff[t][:], a_sb[t][:].indirect(n1_t[:]), a_copy[t][:], ALU.subtract)
+            else:
+                nc.vector.tensor_tensor(diff[t][:], a_copy[t][:], a_sb[t][:, :S], ALU.subtract)
 
+        nc.vector.tensor_scalar(neg_gn[:], gn_t[:], -1.0, None, ALU.mult)
         deal(w2_dealt, w2_raw)
         deal(w1_dealt, w1_raw)
         deal(ws_dealt, ws_raw)
@@ -193,9 +202,7 @@ def tile_picked_kjgdifoddsdet_none_po_kernel(
                     rhs=z2_w[:, cols(h)].bitcast(FP8X4), rhs_scale=z2_s[:, cols(h)], start=True, stop=False,
                 )
 
-        hs = [sb(f"hs{t}", [P, 2 * S], F32) for t in range(PACK)]
-        for window in hs:
-            nc.gpsimd.memset(window[:, S:], 0.0)
+        hs = ex
         root = math.sqrt(0.75)
         sig = sb("sig", [P, PACK, S], F32, f"sums{PACK - 1}")
         for k, (lo, hi) in enumerate(((0, HALF), (HALF, HALF + QUARTER), (HALF + QUARTER, S))):
@@ -229,8 +236,8 @@ def tile_picked_kjgdifoddsdet_none_po_kernel(
         res = [sb(f"res{h}", [P, PACK, HALF], F32) for h in range(2)]
         steps = [(0, 0, HALF), (0, HALF, S), (1, 0, S), (2, 0, S), (3, 0, HALF), (3, HALF, S)]
         h6 = [sb(f"h6_{t}", [P, S], F32, f"ex4_{t}") for t in range(PACK)]
-        h8 = [sb(f"h8_{t}", [P, S], F32, f"ex_copy{t}") for t in range(PACK)]
-        h9 = sb("h9", [P, S], F32)
+        h8 = [sb(f"h8_{t}", [P, S], F32, f"diff{t}") for t in range(PACK)]
+        h9 = {t: sb(f"h9_{t}", [P, S], F32, f"logs{t}") for t in range(FUSED_C, PACK)}
         p67 = [sb(f"p67_{t}", [P, S], F32, f"a_copy{t}") for t in range(PACK)]
         p89 = [sb(f"p89_{t}", [P, S], F32, f"den_g{t}") for t in range(PACK)]
 
@@ -238,9 +245,9 @@ def tile_picked_kjgdifoddsdet_none_po_kernel(
             nc.scalar.activation(h6[t][:, lo:hi], hs[t][:].indirect(part(n6_t, lo, hi)), ACT.Copy)
             nc.scalar.activation(h8[t][:, lo:hi], hs[t][:].indirect(part(n8_t, lo, hi)), ACT.Copy)
             nc.vector.tensor_tensor(p67[t][:, lo:hi], hs[t][:].indirect(part(n7_t, lo, hi)), h6[t][:, lo:hi], ALU.mult)
-            if t == PACK - 1:
-                nc.scalar.activation(h9[:, lo:hi], hs[t][:].indirect(part(n9_t, lo, hi)), ACT.Copy)
-                nc.vector.tensor_tensor(p89[t][:, lo:hi], h9[:, lo:hi], h8[t][:, lo:hi], ALU.mult)
+            if t >= FUSED_C:
+                nc.scalar.activation(h9[t][:, lo:hi], hs[t][:].indirect(part(n9_t, lo, hi)), ACT.Copy)
+                nc.vector.tensor_tensor(p89[t][:, lo:hi], h9[t][:, lo:hi], h8[t][:, lo:hi], ALU.mult)
             else:
                 nc.vector.tensor_tensor(p89[t][:, lo:hi], hs[t][:].indirect(part(n9_t, lo, hi)), h8[t][:, lo:hi], ALU.mult)
 
@@ -249,11 +256,13 @@ def tile_picked_kjgdifoddsdet_none_po_kernel(
                 nc.vector.tensor_tensor(res[h][:, t, :], p67[t][:, cols(h)], p89[t][:, cols(h)], ALU.subtract)
                 nc.sync.dma_start(out_rows[:, t, cols(h)], res[h][:, t, :])
 
-        for k in range(len(steps) + 1):
-            if k < len(steps):
-                products(*steps[k])
+        for k, step in enumerate(steps[:-1]):
+            products(*step)
             if k > 0:
                 finish(*steps[k - 1])
+        finish(*steps[-2])
+        products(*steps[-1])
+        finish(*steps[-1])
         for h in range(2):
             o_bf = sb(f"o_bf{h}", [P, PACK * HALF], BF16)
             o_w = sb(f"o_w{h}", [P, HALF], U32)

@@ -20,9 +20,8 @@ T = 1024
 G = 2048
 HALF = S // 2
 QUARTER = S // 4
-LIST_COLS = S // 16
-FUSED_A = 3
-FUSED_C = 3
+GROUP = 16
+FUSED = 3
 FLOPS = 4 * 2 * 512 * 512 * 512
 
 
@@ -35,48 +34,50 @@ def tile_picked_kjgdifoddsdet_none_po_kernel(
         keep = ctx.enter_context(tc.tile_pool(name="keep", bufs=1))
         psum = ctx.enter_context(tc.psum_pool(name="psum", bufs=1))
 
-        def sb(name, shape, dtype, tag=None):
-            return keep.tile(shape, dtype, name=name, tag=tag or name, align_bytes=64)
+        def sb(name, shape, dtype, after=None):
+            return keep.tile(shape, dtype, name=name, tag=after or name, align_bytes=64)
 
         def load_list(name, src):
-            tile = sb(name, [P, LIST_COLS], U16)
+            tile = sb(name, [P, S // GROUP], U16)
             nc.sync.dma_start(tile[:], src)
             return tile
 
-        def load_words(name, src, cols, tag=None):
-            tile = sb(name, [P, cols], U32, tag)
+        def load_words(name, src, width, after=None):
+            tile = sb(name, [P, width], U32, after)
             nc.sync.dma_start(tile[:].bitcast(I32), src[0].rearrange("p n t -> p (n t)").bitcast(I32))
             return tile
 
         def deal(dst, src):
             nc.vector.tensor_copy(dst[:].rearrange("p (t m) -> p t m", t=PACK), src[:].rearrange("p (m t) -> p t m", t=PACK))
 
-        def part(lst, lo, hi):
-            return lst[:, lo // 16 : hi // 16]
-
-        def cols(h):
-            return slice(h * HALF, (h + 1) * HALF)
-
-        def rows(t):
-            return slice(t * P, (t + 1) * P)
+        def place_rows(queue, plane, src):
+            for r in range(PACK):
+                queue.dma_start(plane[r:P:32, :].bitcast(I32), src[8 * r : P : 32, :].bitcast(I32))
 
         def weave(dst, src, copy=nc.vector.tensor_copy):
-            copy(
-                dst[:].rearrange("p (c i t) -> p c t i", i=4, t=PACK), src[:].rearrange("p t (c i) -> p c t i", i=4)
-            )
+            copy(dst[:].rearrange("p (c i t) -> p c t i", i=4, t=PACK), src[:].rearrange("p t (c i) -> p c t i", i=4))
+
+        def entries(lst, lo, hi):
+            return lst[:, lo // GROUP : hi // GROUP]
+
+        def half(h):
+            return slice(h * HALF, (h + 1) * HALF)
+
+        def dealt(t):
+            return slice(t * P, (t + 1) * P)
 
         ds_table = sb("ds_table", [P, G], U8)
         xs_table = sb("xs_table", [P, T], U8)
-        planes_b = sb("planes_b", [P, 2 * S], U8)
+        placed_b = sb("placed_b", [P, 2 * S], U8)
         plane_a = sb("plane_a", [P, S], U8)
         nc.vector.memset(ds_table[:, : G // 2].bitcast(I32), 0)
         nc.gpsimd.memset(ds_table[:, G // 2 :].bitcast(I32), 0)
         nc.vector.memset(xs_table[:].bitcast(I32), 0)
-        nc.gpsimd.memset(planes_b[:].bitcast(I32), 0)
+        nc.gpsimd.memset(placed_b[:].bitcast(I32), 0)
         nc.gpsimd.memset(plane_a[:].bitcast(I32), 0)
-        ex = [sb(f"ex{t}", [P, 2 * S], F32) for t in range(PACK)]
-        a_sb = [sb(f"a_sb{t}", [P, 2 * S], F32) for t in range(PACK)]
-        for window in ex:
+        ex_win = [sb(f"ex_win{t}", [P, 2 * S], F32) for t in range(PACK)]
+        a_win = [sb(f"a_win{t}", [P, 2 * S], F32) for t in range(PACK)]
+        for window in ex_win:
             nc.vector.memset(window[:, S:], 0.0)
 
         k1_t = load_list("k1_t", k1)
@@ -96,96 +97,96 @@ def tile_picked_kjgdifoddsdet_none_po_kernel(
         n8_t = load_list("n8_t", n8)
         n9_t = load_list("n9_t", n9)
 
-        def place_rows(queue, plane, src):
-            for r in range(4):
-                queue.dma_start(plane[r:P:32, :].bitcast(I32), src[8 * r : P : 32, :].bitcast(I32))
-
-        ds_picked = sb("ds_picked", [P, S], U8)
-        xs_b = sb("xs_b", [P, S], U8)
-        rows_b = sb("rows_b", [P, 2 * S], U8)
+        ds_plane = sb("ds_plane", [P, S], U8)
+        picked_b = sb("picked_b", [P, 2 * S], U8)
         xw_b = sb("xw_b", [P, S], U32)
         dw_picked = sb("dw_picked", [P, S], U32)
         dw_dealt = sb("dw_dealt", [P, S], U32)
-        nc.vector.tensor_copy(ds_picked[:], ds_table[:].indirect(k1_t[:]))
-        nc.vector.tensor_copy(xs_b[:], xs_table[:].indirect(two_t[:]))
-        deal(rows_b[:, :S], ds_picked)
-        nc.vector.tensor_copy(rows_b[:, S:].bitcast(I32), xs_b[:].bitcast(I32))
-        place_rows(nc.scalar, planes_b, rows_b)
+        nc.vector.tensor_copy(picked_b[:, :S], ds_table[:].indirect(k1_t[:]))
+        nc.vector.tensor_copy(picked_b[:, S:], xs_table[:].indirect(two_t[:]))
+        place_rows(nc.scalar, placed_b, picked_b)
         nc.vector.tensor_copy(xw_b[:], xw_table[:].indirect(two_t[:]))
         nc.vector.tensor_copy(dw_picked[:], dw_table[:].indirect(k1_t[:]))
         deal(dw_dealt, dw_picked)
-        xs_a = sb("xs_a", [P, S], U8, "dw_table")
+        deal(ds_plane, placed_b[:, :S])
+        picked_a = sb("picked_a", [P, S], U8, "dw_table")
         xw_a = sb("xw_a", [P, S], U32, "dw_picked")
-        nc.vector.tensor_copy(xs_a[:], xs_table[:].indirect(offs_t[:]))
-        place_rows(nc.sync, plane_a, xs_a)
+        nc.vector.tensor_copy(picked_a[:], xs_table[:].indirect(offs_t[:]))
+        place_rows(nc.sync, plane_a, picked_a)
         nc.vector.tensor_copy(xw_a[:], xw_table[:].indirect(offs_t[:]))
 
-        def scores(name, words, scales):
+        def scores(name, words, plane):
             banks = [psum.tile([P, S], F32, name=f"{name}{t}", tag=f"{name}{t}") for t in range(PACK)]
             for t in range(PACK):
                 nc.tensor.matmul_mx(
-                    out=banks[t][:], lhsT=dw_dealt[:, rows(t)].bitcast(FP8X4), lhsT_scale=planes_b[:, rows(t)],
-                    rhs=words[:].bitcast(FP8X4), rhs_scale=scales, start=True, stop=True,
+                    out=banks[t][:], lhsT=dw_dealt[:, dealt(t)].bitcast(FP8X4), lhsT_scale=ds_plane[:, dealt(t)],
+                    rhs=words[:].bitcast(FP8X4), rhs_scale=plane, start=True, stop=True,
                 )
             return banks
 
-        b_banks = scores("bank_b", xw_b, planes_b[:, S:])
+        b_banks = scores("bank_b", xw_b, placed_b[:, S:])
         a_banks = scores("bank_a", xw_a, plane_a[:])
 
-        ex_copy = [a_sb[t][:, S:] for t in range(PACK)]
-        a_copy = [sb(f"a_copy{t}", [P, S], F32) for t in range(PACK)]
-        ex4 = [sb(f"ex4_{t}", [P, S], F32) for t in range(PACK)]
+        ex_copy = [a_win[t][:, S:] for t in range(PACK)]
+        a_copy = [sb(f"a_copy{t}", [P, S], F32) for t in range(FUSED)]
+        a_n1 = {t: sb(f"a_copy{t}", [P, S], F32) for t in range(FUSED, PACK)}
+        ex_n4 = [sb(f"ex_n4_{t}", [P, S], F32) for t in range(PACK)]
         sums = [sb(f"sums{t}", [P, 2 * S], F32) for t in range(PACK)]
         logs = [sb(f"logs{t}", [P, 2 * S], F32) for t in range(PACK)]
-        den_g = [sb(f"den_g{t}", [P, S], F32) for t in range(PACK)]
+        gm_log_den = [sb(f"gm_log_den{t}", [P, S], F32) for t in range(PACK)]
         diff = [sb(f"diff{t}", [P, S], F32) for t in range(PACK)]
         for t in range(PACK):
-            nc.scalar.activation(ex[t][:, :S], b_banks[t][:], ACT.Exp, scale=0.5 * 0.0625)
-            nc.sync.dma_start(ex_copy[t], ex[t][:, :S])
+            nc.scalar.activation(ex_win[t][:, :S], b_banks[t][:], ACT.Exp, scale=0.5 * 0.0625)
+            nc.sync.dma_start(ex_copy[t], ex_win[t][:, :S])
         for t in range(PACK):
             if t == 0:
-                nc.vector.tensor_copy(ex4[t][:], ex[t][:].indirect(n4_t[:]))
+                nc.vector.tensor_copy(ex_n4[t][:], ex_win[t][:].indirect(n4_t[:]))
             else:
-                nc.scalar.activation(ex4[t][:], ex[t][:].indirect(n4_t[:]), ACT.Copy)
-            nc.vector.tensor_tensor(sums[t][:, S:], ex[t][:].indirect(n5_t[:]), ex4[t][:], ALU.add)
-            nc.vector.tensor_tensor(sums[t][:, :S], ex[t][:].indirect(n3_t[:]), ex_copy[t], ALU.add)
+                nc.scalar.activation(ex_n4[t][:], ex_win[t][:].indirect(n4_t[:]), ACT.Copy)
+            nc.vector.tensor_tensor(sums[t][:, S:], ex_win[t][:].indirect(n5_t[:]), ex_n4[t][:], ALU.add)
+            nc.vector.tensor_tensor(sums[t][:, :S], ex_win[t][:].indirect(n3_t[:]), ex_copy[t], ALU.add)
+
         gm_t = sb("gm_t", [P, PACK], F32, "xw_b")
         nc.sync.dma_start(gm_t[:], gm.rearrange("(p t) o -> p (t o)", t=PACK))
         gn_t = sb("gn_t", [P, PACK], F32, "xw_table")
         nc.sync.dma_start(gn_t[:], gn.rearrange("(p t) o -> p (t o)", t=PACK))
         ws_raw = sb("ws_raw", [P, S], U8, "dw_table")
         nc.vector.memset(ws_raw[:].bitcast(I32), 0)
-        w2_raw = load_words("w2_raw", w2_words, S, "ex4_0")
+        w2_raw = load_words("w2_raw", w2_words, S, "ex_n4_0")
         w1_raw = load_words("w1_raw", w1_words, S, "dw_picked")
-        for r in range(4):
-            nc.sync.dma_start(ws_raw[4 + r : P : 32, :].bitcast(I32), w2_scales[0].bitcast(I32)[r:16:4, :])
-            nc.sync.dma_start(ws_raw[r:P:32, :].bitcast(I32), w1_scales[0].bitcast(I32)[r:16:4, :])
+        for r in range(PACK):
+            nc.sync.dma_start(ws_raw[PACK + r : P : 32, :].bitcast(I32), w2_scales[0].bitcast(I32)[r:16:PACK, :])
+            nc.sync.dma_start(ws_raw[r:P:32, :].bitcast(I32), w1_scales[0].bitcast(I32)[r:16:PACK, :])
         w1_dealt = sb("w1_dealt", [P, S], U32)
         w2_dealt = sb("w2_dealt", [P, S], U32)
         ws_dealt = sb("ws_dealt", [P, S], U8)
         neg_gn = sb("neg_gn", [P, PACK], F32)
+
         for t in range(PACK):
-            nc.scalar.activation(a_sb[t][:, :S], a_banks[t][:], ACT.Copy, scale=0.0625)
-            if t < FUSED_A:
-                nc.sync.dma_start(a_copy[t][:], a_sb[t][:, :S])
-        for t in range(FUSED_A, PACK):
-            nc.scalar.activation(a_copy[t][:], a_sb[t][:].indirect(n1_t[:]), ACT.Copy)
+            nc.scalar.activation(a_win[t][:, :S], a_banks[t][:], ACT.Copy, scale=0.0625)
+            if t < FUSED:
+                nc.sync.dma_start(a_copy[t][:], a_win[t][:, :S])
+        for t in range(FUSED, PACK):
+            nc.scalar.activation(a_n1[t][:], a_win[t][:].indirect(n1_t[:]), ACT.Copy)
         for t in range(PACK):
             nc.scalar.activation(logs[t][:], sums[t][:], ACT.Ln)
-            nc.scalar.activation(den_g[t][:], logs[t][:, S:], ACT.Copy, scale=gm_t[:, t : t + 1])
+            nc.scalar.activation(gm_log_den[t][:], logs[t][:, S:], ACT.Copy, scale=gm_t[:, t : t + 1])
         for t in range(PACK):
-            if t < FUSED_A:
-                nc.vector.tensor_tensor(diff[t][:], a_sb[t][:].indirect(n1_t[:]), a_copy[t][:], ALU.subtract)
+            if t < FUSED:
+                nc.vector.tensor_tensor(diff[t][:], a_win[t][:].indirect(n1_t[:]), a_copy[t][:], ALU.subtract)
             else:
-                nc.vector.tensor_tensor(diff[t][:], a_copy[t][:], a_sb[t][:, :S], ALU.subtract)
+                nc.vector.tensor_tensor(diff[t][:], a_n1[t][:], a_win[t][:, :S], ALU.subtract)
 
         nc.vector.tensor_scalar(neg_gn[:], gn_t[:], -1.0, None, ALU.mult)
         deal(w2_dealt, w2_raw)
         deal(w1_dealt, w1_raw)
         deal(ws_dealt, ws_raw)
+
         z2 = sb("z2", [P, PACK, S], F32)
         for t in range(PACK):
-            nc.vector.scalar_tensor_tensor(z2[:, t, :], logs[t][:, :S], gm_t[:, t : t + 1], den_g[t][:], ALU.mult, ALU.subtract)
+            nc.vector.scalar_tensor_tensor(
+                z2[:, t, :], logs[t][:, :S], gm_t[:, t : t + 1], gm_log_den[t][:], ALU.mult, ALU.subtract
+            )
         z2_bf = sb("z2_bf", [P, PACK * S], BF16)
         z2_w = sb("z2_w", [P, S], U32)
         z2_s = sb("z2_s", [P, S], U8)
@@ -198,64 +199,67 @@ def tile_picked_kjgdifoddsdet_none_po_kernel(
         for h in range(2):
             for t in range(PACK):
                 nc.tensor.matmul_mx(
-                    out=h_banks[h][t][:], lhsT=w2_dealt[:, rows(t)].bitcast(FP8X4), lhsT_scale=ws_dealt[4:P, rows(t)],
-                    rhs=z2_w[:, cols(h)].bitcast(FP8X4), rhs_scale=z2_s[:, cols(h)], start=True, stop=False,
+                    out=h_banks[h][t][:], lhsT=w2_dealt[:, dealt(t)].bitcast(FP8X4), lhsT_scale=ws_dealt[PACK:P, dealt(t)],
+                    rhs=z2_w[:, half(h)].bitcast(FP8X4), rhs_scale=z2_s[:, half(h)], start=True, stop=False,
                 )
 
-        hs = ex
-        root = math.sqrt(0.75)
         sig = sb("sig", [P, PACK, S], F32, f"sums{PACK - 1}")
-        for k, (lo, hi) in enumerate(((0, HALF), (HALF, HALF + QUARTER), (HALF + QUARTER, S))):
+        for lo, hi in ((0, HALF), (HALF, HALF + QUARTER), (HALF + QUARTER, S)):
             h, width = lo // HALF, hi - lo
-            z = sb(f"z{k}", [P, PACK, width], F32)
+            z = sb(f"z{lo}", [P, PACK, width], F32)
             for t in range(PACK):
-                nc.scalar.activation(sig[:, t, lo:hi], a_sb[t][:].indirect(part(n2_t, lo, hi)), ACT.Sigmoid)
-                nc.vector.scalar_tensor_tensor(z[:, t, :], diff[t][:, lo:hi], neg_gn[:, t : t + 1], sig[:, t, lo:hi], ALU.mult, ALU.mult)
-            z_bf = sb(f"z_bf{k}", [P, PACK * width], BF16)
-            z_w = sb(f"z_w{k}", [P, width], U32)
-            z_s = sb(f"z_s{k}", [P, width], U8)
+                nc.scalar.activation(sig[:, t, lo:hi], a_win[t][:].indirect(entries(n2_t, lo, hi)), ACT.Sigmoid)
+                nc.vector.scalar_tensor_tensor(
+                    z[:, t, :], diff[t][:, lo:hi], neg_gn[:, t : t + 1], sig[:, t, lo:hi], ALU.mult, ALU.mult
+                )
+            z_bf = sb(f"z_bf{lo}", [P, PACK * width], BF16)
+            z_w = sb(f"z_w{lo}", [P, width], U32)
+            z_s = sb(f"z_s{lo}", [P, width], U8)
             weave(z_bf, z)
             nc.vector.quantize_mx(out=z_w[:].bitcast(FP8X4), scales=z_s[:], in_=z_bf[:])
             for t in range(PACK):
                 nc.tensor.matmul_mx(
-                    out=h_banks[h][t][:, lo - h * HALF : hi - h * HALF], lhsT=w1_dealt[:, rows(t)].bitcast(FP8X4),
-                    lhsT_scale=ws_dealt[:, rows(t)], rhs=z_w[:].bitcast(FP8X4), rhs_scale=z_s[:],
+                    out=h_banks[h][t][:, lo - h * HALF : hi - h * HALF], lhsT=w1_dealt[:, dealt(t)].bitcast(FP8X4),
+                    lhsT_scale=ws_dealt[:, dealt(t)], rhs=z_w[:].bitcast(FP8X4), rhs_scale=z_s[:],
                     start=False, stop=(hi % HALF == 0),
                 )
+
+        h_win = ex_win
+        root = math.sqrt(0.75)
         for h in range(2):
             for t in range(PACK):
                 if h == 1 and t > 0:
-                    nc.vector.tensor_scalar(hs[t][:, cols(h)], h_banks[h][t][:], root, None, ALU.mult)
+                    nc.vector.tensor_scalar(h_win[t][:, half(h)], h_banks[h][t][:], root, None, ALU.mult)
                 else:
-                    nc.scalar.activation(hs[t][:, cols(h)], h_banks[h][t][:], ACT.Copy, scale=root)
+                    nc.scalar.activation(h_win[t][:, half(h)], h_banks[h][t][:], ACT.Copy, scale=root)
 
         out_rows = out_0.rearrange("(p t) j -> p t j", t=PACK)
         out_words = out_1[0].rearrange("p n t -> p (n t)").bitcast(I32)
         out_scales = out_2[0].bitcast(I32)
         o_s = sb("o_s", [P, S], U8)
         res = [sb(f"res{h}", [P, PACK, HALF], F32) for h in range(2)]
-        steps = [(0, 0, HALF), (0, HALF, S), (1, 0, S), (2, 0, S), (3, 0, HALF), (3, HALF, S)]
-        h6 = [sb(f"h6_{t}", [P, S], F32, f"ex4_{t}") for t in range(PACK)]
-        h8 = [sb(f"h8_{t}", [P, S], F32, f"diff{t}") for t in range(PACK)]
-        h9 = {t: sb(f"h9_{t}", [P, S], F32, f"logs{t}") for t in range(FUSED_C, PACK)}
+        h_n6 = [sb(f"h_n6_{t}", [P, S], F32, f"ex_n4_{t}") for t in range(PACK)]
+        h_n8 = [sb(f"h_n8_{t}", [P, S], F32, f"diff{t}") for t in range(PACK)]
+        h_n9 = {t: sb(f"h_n9_{t}", [P, S], F32, f"logs{t}") for t in range(FUSED, PACK)}
         p67 = [sb(f"p67_{t}", [P, S], F32, f"a_copy{t}") for t in range(PACK)]
-        p89 = [sb(f"p89_{t}", [P, S], F32, f"den_g{t}") for t in range(PACK)]
+        p89 = [sb(f"p89_{t}", [P, S], F32, f"gm_log_den{t}") for t in range(PACK)]
 
         def products(t, lo, hi):
-            nc.scalar.activation(h6[t][:, lo:hi], hs[t][:].indirect(part(n6_t, lo, hi)), ACT.Copy)
-            nc.scalar.activation(h8[t][:, lo:hi], hs[t][:].indirect(part(n8_t, lo, hi)), ACT.Copy)
-            nc.vector.tensor_tensor(p67[t][:, lo:hi], hs[t][:].indirect(part(n7_t, lo, hi)), h6[t][:, lo:hi], ALU.mult)
-            if t >= FUSED_C:
-                nc.scalar.activation(h9[t][:, lo:hi], hs[t][:].indirect(part(n9_t, lo, hi)), ACT.Copy)
-                nc.vector.tensor_tensor(p89[t][:, lo:hi], h9[t][:, lo:hi], h8[t][:, lo:hi], ALU.mult)
+            nc.scalar.activation(h_n6[t][:, lo:hi], h_win[t][:].indirect(entries(n6_t, lo, hi)), ACT.Copy)
+            nc.scalar.activation(h_n8[t][:, lo:hi], h_win[t][:].indirect(entries(n8_t, lo, hi)), ACT.Copy)
+            nc.vector.tensor_tensor(p67[t][:, lo:hi], h_win[t][:].indirect(entries(n7_t, lo, hi)), h_n6[t][:, lo:hi], ALU.mult)
+            if t < FUSED:
+                nc.vector.tensor_tensor(p89[t][:, lo:hi], h_win[t][:].indirect(entries(n9_t, lo, hi)), h_n8[t][:, lo:hi], ALU.mult)
             else:
-                nc.vector.tensor_tensor(p89[t][:, lo:hi], hs[t][:].indirect(part(n9_t, lo, hi)), h8[t][:, lo:hi], ALU.mult)
+                nc.scalar.activation(h_n9[t][:, lo:hi], h_win[t][:].indirect(entries(n9_t, lo, hi)), ACT.Copy)
+                nc.vector.tensor_tensor(p89[t][:, lo:hi], h_n9[t][:, lo:hi], h_n8[t][:, lo:hi], ALU.mult)
 
         def finish(t, lo, hi):
             for h in range(lo // HALF, hi // HALF):
-                nc.vector.tensor_tensor(res[h][:, t, :], p67[t][:, cols(h)], p89[t][:, cols(h)], ALU.subtract)
-                nc.sync.dma_start(out_rows[:, t, cols(h)], res[h][:, t, :])
+                nc.vector.tensor_tensor(res[h][:, t, :], p67[t][:, half(h)], p89[t][:, half(h)], ALU.subtract)
+                nc.sync.dma_start(out_rows[:, t, half(h)], res[h][:, t, :])
 
+        steps = [(0, 0, HALF), (0, HALF, S), (1, 0, S), (2, 0, S), (3, 0, HALF), (3, HALF, S)]
         for k, step in enumerate(steps[:-1]):
             products(*step)
             if k > 0:
@@ -263,12 +267,13 @@ def tile_picked_kjgdifoddsdet_none_po_kernel(
         finish(*steps[-2])
         products(*steps[-1])
         finish(*steps[-1])
+
         for h in range(2):
             o_bf = sb(f"o_bf{h}", [P, PACK * HALF], BF16)
             o_w = sb(f"o_w{h}", [P, HALF], U32)
             weave(o_bf, res[h], nc.vector.tensor_copy if h else nc.scalar.copy)
-            nc.vector.quantize_mx(out=o_w[:].bitcast(FP8X4), scales=o_s[:, cols(h)], in_=o_bf[:])
-            nc.sync.dma_start(out_words[:, cols(h)], o_w[:].bitcast(I32))
-        for r in range(4):
+            nc.vector.quantize_mx(out=o_w[:].bitcast(FP8X4), scales=o_s[:, half(h)], in_=o_bf[:])
+            nc.sync.dma_start(out_words[:, half(h)], o_w[:].bitcast(I32))
+        for r in range(PACK):
             queue = nc.scalar if r % 2 else nc.sync
-            queue.dma_start(out_scales[r:16:4, :], o_s[r:P:32, :].bitcast(I32))
+            queue.dma_start(out_scales[r:16:PACK, :], o_s[r:P:32, :].bitcast(I32))

import math
from contextlib import ExitStack

import concourse.mybir as mybir

F32 = mybir.dt.float32
BF16 = mybir.dt.bfloat16
I32 = mybir.dt.int32
U32 = mybir.dt.uint32
U16 = mybir.dt.uint16
U8 = mybir.dt.uint8
FP8X4 = mybir.dt.float8_e4m3fn_x4
ALU = mybir.AluOpType
ACT = mybir.ActivationFunctionType

P = 128
PACK = 4
S = 512
T = 1024
G = 2048
HALF = S // 2
QUARTER = S // 4
GROUP = 16
FUSED = 3
FLOPS = 4 * 2 * 512 * 512 * 512


def tile_picked_kjgdifoddsdet_none_po_kernel(
    tc, x_words, x_scales, d_words, d_scales, gn, gm, w1_words, w1_scales, w2_words, w2_scales,
    offs, k1, two, n1, n2, n3, n4, n5, n6, n7, n8, n9, out_0, out_1, out_2,
):
    nc = tc.nc
    with ExitStack() as ctx:
        keep = ctx.enter_context(tc.tile_pool(name="keep", bufs=1))
        psum = ctx.enter_context(tc.psum_pool(name="psum", bufs=1))

        def sb(name, shape, dtype, after=None):
            return keep.tile(shape, dtype, name=name, tag=after or name, align_bytes=64)

        def load_list(name, src):
            tile = sb(name, [P, S // GROUP], U16)
            nc.sync.dma_start(tile[:], src)
            return tile

        def load_words(name, src, width, after=None):
            tile = sb(name, [P, width], U32, after)
            nc.sync.dma_start(tile[:].bitcast(I32), src[0].rearrange("p n t -> p (n t)").bitcast(I32))
            return tile

        def deal(dst, src):
            nc.vector.tensor_copy(dst[:].rearrange("p (t m) -> p t m", t=PACK), src[:].rearrange("p (m t) -> p t m", t=PACK))

        def place_rows(queue, plane, src):
            for r in range(PACK):
                queue.dma_start(plane[r:P:32, :].bitcast(I32), src[8 * r : P : 32, :].bitcast(I32))

        def weave(dst, src, copy=nc.vector.tensor_copy):
            copy(dst[:].rearrange("p (c i t) -> p c t i", i=4, t=PACK), src[:].rearrange("p t (c i) -> p c t i", i=4))

        def entries(lst, lo, hi):
            return lst[:, lo // GROUP : hi // GROUP]

        def half(h):
            return slice(h * HALF, (h + 1) * HALF)

        def dealt(t):
            return slice(t * P, (t + 1) * P)

        ds_table = sb("ds_table", [P, G], U8)
        xs_table = sb("xs_table", [P, T], U8)
        placed_b = sb("placed_b", [P, 2 * S], U8)
        plane_a = sb("plane_a", [P, S], U8)
        nc.vector.memset(ds_table[:, : G // 2].bitcast(I32), 0)
        nc.gpsimd.memset(ds_table[:, G // 2 :].bitcast(I32), 0)
        nc.vector.memset(xs_table[:].bitcast(I32), 0)
        nc.gpsimd.memset(placed_b[:].bitcast(I32), 0)
        nc.gpsimd.memset(plane_a[:].bitcast(I32), 0)
        ex_win = [sb(f"ex_win{t}", [P, 2 * S], F32) for t in range(PACK)]
        a_win = [sb(f"a_win{t}", [P, 2 * S], F32) for t in range(PACK)]
        for window in ex_win:
            nc.vector.memset(window[:, S:], 0.0)

        k1_t = load_list("k1_t", k1)
        nc.sync.dma_start(ds_table[0:P:8, :].bitcast(I32), d_scales[0].bitcast(I32))
        two_t = load_list("two_t", two)
        nc.sync.dma_start(xs_table[0:P:8, :].bitcast(I32), x_scales[0].bitcast(I32))
        offs_t = load_list("offs_t", offs)
        n4_t = load_list("n4_t", n4)
        xw_table = load_words("xw_table", x_words, T)
        dw_table = load_words("dw_table", d_words, G)
        n5_t = load_list("n5_t", n5)
        n3_t = load_list("n3_t", n3)
        n1_t = load_list("n1_t", n1)
        n2_t = load_list("n2_t", n2)
        n6_t = load_list("n6_t", n6)
        n7_t = load_list("n7_t", n7)
        n8_t = load_list("n8_t", n8)
        n9_t = load_list("n9_t", n9)

        ds_plane = sb("ds_plane", [P, S], U8)
        picked_b = sb("picked_b", [P, 2 * S], U8)
        xw_b = sb("xw_b", [P, S], U32)
        dw_picked = sb("dw_picked", [P, S], U32)
        dw_dealt = sb("dw_dealt", [P, S], U32)
        nc.vector.tensor_copy(picked_b[:, :S], ds_table[:].indirect(k1_t[:]))
        nc.vector.tensor_copy(picked_b[:, S:], xs_table[:].indirect(two_t[:]))
        place_rows(nc.scalar, placed_b, picked_b)
        nc.vector.tensor_copy(xw_b[:], xw_table[:].indirect(two_t[:]))
        nc.vector.tensor_copy(dw_picked[:], dw_table[:].indirect(k1_t[:]))
        deal(dw_dealt, dw_picked)
        deal(ds_plane, placed_b[:, :S])
        picked_a = sb("picked_a", [P, S], U8, "dw_table")
        xw_a = sb("xw_a", [P, S], U32, "dw_picked")
        nc.vector.tensor_copy(picked_a[:], xs_table[:].indirect(offs_t[:]))
        place_rows(nc.sync, plane_a, picked_a)
        nc.vector.tensor_copy(xw_a[:], xw_table[:].indirect(offs_t[:]))

        def scores(name, words, plane):
            banks = [psum.tile([P, S], F32, name=f"{name}{t}", tag=f"{name}{t}") for t in range(PACK)]
            for t in range(PACK):
                nc.tensor.matmul_mx(
                    out=banks[t][:], lhsT=dw_dealt[:, dealt(t)].bitcast(FP8X4), lhsT_scale=ds_plane[:, dealt(t)],
                    rhs=words[:].bitcast(FP8X4), rhs_scale=plane, start=True, stop=True,
                )
            return banks

        b_banks = scores("bank_b", xw_b, placed_b[:, S:])
        a_banks = scores("bank_a", xw_a, plane_a[:])

        ex_copy = [a_win[t][:, S:] for t in range(PACK)]
        a_copy = [sb(f"a_copy{t}", [P, S], F32) for t in range(FUSED)]
        a_n1 = {t: sb(f"a_copy{t}", [P, S], F32) for t in range(FUSED, PACK)}
        ex_n4 = [sb(f"ex_n4_{t}", [P, S], F32) for t in range(PACK)]
        sums = [sb(f"sums{t}", [P, 2 * S], F32) for t in range(PACK)]
        logs = [sb(f"logs{t}", [P, 2 * S], F32) for t in range(PACK)]
        gm_log_den = [sb(f"gm_log_den{t}", [P, S], F32) for t in range(PACK)]
        diff = [sb(f"diff{t}", [P, S], F32) for t in range(PACK)]
        for t in range(PACK):
            nc.scalar.activation(ex_win[t][:, :S], b_banks[t][:], ACT.Exp, scale=0.5 * 0.0625)
            nc.sync.dma_start(ex_copy[t], ex_win[t][:, :S])
        for t in range(PACK):
            if t == 0:
                nc.vector.tensor_copy(ex_n4[t][:], ex_win[t][:].indirect(n4_t[:]))
            else:
                nc.scalar.activation(ex_n4[t][:], ex_win[t][:].indirect(n4_t[:]), ACT.Copy)
            nc.vector.tensor_tensor(sums[t][:, S:], ex_win[t][:].indirect(n5_t[:]), ex_n4[t][:], ALU.add)
            nc.vector.tensor_tensor(sums[t][:, :S], ex_win[t][:].indirect(n3_t[:]), ex_copy[t], ALU.add)

        gm_t = sb("gm_t", [P, PACK], F32, "xw_b")
        nc.sync.dma_start(gm_t[:], gm.rearrange("(p t) o -> p (t o)", t=PACK))
        gn_t = sb("gn_t", [P, PACK], F32, "xw_table")
        nc.sync.dma_start(gn_t[:], gn.rearrange("(p t) o -> p (t o)", t=PACK))
        ws_raw = sb("ws_raw", [P, S], U8, "dw_table")
        nc.vector.memset(ws_raw[:].bitcast(I32), 0)
        w2_raw = load_words("w2_raw", w2_words, S, "ex_n4_0")
        w1_raw = load_words("w1_raw", w1_words, S, "dw_picked")
        for r in range(PACK):
            nc.sync.dma_start(ws_raw[PACK + r : P : 32, :].bitcast(I32), w2_scales[0].bitcast(I32)[r:16:PACK, :])
            nc.sync.dma_start(ws_raw[r:P:32, :].bitcast(I32), w1_scales[0].bitcast(I32)[r:16:PACK, :])
        w1_dealt = sb("w1_dealt", [P, S], U32)
        w2_dealt = sb("w2_dealt", [P, S], U32)
        ws_dealt = sb("ws_dealt", [P, S], U8)
        neg_gn = sb("neg_gn", [P, PACK], F32)

        for t in range(PACK):
            nc.scalar.activation(a_win[t][:, :S], a_banks[t][:], ACT.Copy, scale=0.0625)
            if t < FUSED:
                nc.sync.dma_start(a_copy[t][:], a_win[t][:, :S])
        for t in range(FUSED, PACK):
            nc.scalar.activation(a_n1[t][:], a_win[t][:].indirect(n1_t[:]), ACT.Copy)
        for t in range(PACK):
            nc.scalar.activation(logs[t][:], sums[t][:], ACT.Ln)
            nc.scalar.activation(gm_log_den[t][:], logs[t][:, S:], ACT.Copy, scale=gm_t[:, t : t + 1])
        for t in range(PACK):
            if t < FUSED:
                nc.vector.tensor_tensor(diff[t][:], a_win[t][:].indirect(n1_t[:]), a_copy[t][:], ALU.subtract)
            else:
                nc.vector.tensor_tensor(diff[t][:], a_n1[t][:], a_win[t][:, :S], ALU.subtract)

        nc.vector.tensor_scalar(neg_gn[:], gn_t[:], -1.0, None, ALU.mult)
        deal(w2_dealt, w2_raw)
        deal(w1_dealt, w1_raw)
        deal(ws_dealt, ws_raw)

        z2 = sb("z2", [P, PACK, S], F32)
        for t in range(PACK):
            nc.vector.scalar_tensor_tensor(
                z2[:, t, :], logs[t][:, :S], gm_t[:, t : t + 1], gm_log_den[t][:], ALU.mult, ALU.subtract
            )
        z2_bf = sb("z2_bf", [P, PACK * S], BF16)
        z2_w = sb("z2_w", [P, S], U32)
        z2_s = sb("z2_s", [P, S], U8)
        weave(z2_bf, z2)
        nc.vector.quantize_mx(out=z2_w[:].bitcast(FP8X4), scales=z2_s[:], in_=z2_bf[:])

        h_banks = [
            [psum.tile([P, HALF], F32, name=f"h{h}{t}", tag=f"{('bank_b', 'bank_a')[h]}{t}") for t in range(PACK)] for h in range(2)
        ]
        for h in range(2):
            for t in range(PACK):
                nc.tensor.matmul_mx(
                    out=h_banks[h][t][:], lhsT=w2_dealt[:, dealt(t)].bitcast(FP8X4), lhsT_scale=ws_dealt[PACK:P, dealt(t)],
                    rhs=z2_w[:, half(h)].bitcast(FP8X4), rhs_scale=z2_s[:, half(h)], start=True, stop=False,
                )

        sig = sb("sig", [P, PACK, S], F32, f"sums{PACK - 1}")
        for lo, hi in ((0, HALF), (HALF, HALF + QUARTER), (HALF + QUARTER, S)):
            h, width = lo // HALF, hi - lo
            z = sb(f"z{lo}", [P, PACK, width], F32)
            for t in range(PACK):
                nc.scalar.activation(sig[:, t, lo:hi], a_win[t][:].indirect(entries(n2_t, lo, hi)), ACT.Sigmoid)
                nc.vector.scalar_tensor_tensor(
                    z[:, t, :], diff[t][:, lo:hi], neg_gn[:, t : t + 1], sig[:, t, lo:hi], ALU.mult, ALU.mult
                )
            z_bf = sb(f"z_bf{lo}", [P, PACK * width], BF16)
            z_w = sb(f"z_w{lo}", [P, width], U32)
            z_s = sb(f"z_s{lo}", [P, width], U8)
            weave(z_bf, z)
            nc.vector.quantize_mx(out=z_w[:].bitcast(FP8X4), scales=z_s[:], in_=z_bf[:])
            for t in range(PACK):
                nc.tensor.matmul_mx(
                    out=h_banks[h][t][:, lo - h * HALF : hi - h * HALF], lhsT=w1_dealt[:, dealt(t)].bitcast(FP8X4),
                    lhsT_scale=ws_dealt[:, dealt(t)], rhs=z_w[:].bitcast(FP8X4), rhs_scale=z_s[:],
                    start=False, stop=(hi % HALF == 0),
                )

        h_win = ex_win
        root = math.sqrt(0.75)
        for h in range(2):
            for t in range(PACK):
                if h == 1 and t > 0:
                    nc.vector.tensor_scalar(h_win[t][:, half(h)], h_banks[h][t][:], root, None, ALU.mult)
                else:
                    nc.scalar.activation(h_win[t][:, half(h)], h_banks[h][t][:], ACT.Copy, scale=root)

        out_rows = out_0.rearrange("(p t) j -> p t j", t=PACK)
        out_words = out_1[0].rearrange("p n t -> p (n t)").bitcast(I32)
        out_scales = out_2[0].bitcast(I32)
        o_s = sb("o_s", [P, S], U8)
        res = [sb(f"res{h}", [P, PACK, HALF], F32) for h in range(2)]
        h_n6 = [sb(f"h_n6_{t}", [P, S], F32, f"ex_n4_{t}") for t in range(PACK)]
        h_n8 = [sb(f"h_n8_{t}", [P, S], F32, f"diff{t}") for t in range(PACK)]
        h_n9 = {t: sb(f"h_n9_{t}", [P, S], F32, f"logs{t}") for t in range(FUSED, PACK)}
        p67 = [sb(f"p67_{t}", [P, S], F32, f"a_copy{t}") for t in range(PACK)]
        p89 = [sb(f"p89_{t}", [P, S], F32, f"gm_log_den{t}") for t in range(PACK)]

        def products(t, lo, hi):
            nc.scalar.activation(h_n6[t][:, lo:hi], h_win[t][:].indirect(entries(n6_t, lo, hi)), ACT.Copy)
            nc.scalar.activation(h_n8[t][:, lo:hi], h_win[t][:].indirect(entries(n8_t, lo, hi)), ACT.Copy)
            nc.vector.tensor_tensor(p67[t][:, lo:hi], h_win[t][:].indirect(entries(n7_t, lo, hi)), h_n6[t][:, lo:hi], ALU.mult)
            if t < FUSED:
                nc.vector.tensor_tensor(p89[t][:, lo:hi], h_win[t][:].indirect(entries(n9_t, lo, hi)), h_n8[t][:, lo:hi], ALU.mult)
            else:
                nc.scalar.activation(h_n9[t][:, lo:hi], h_win[t][:].indirect(entries(n9_t, lo, hi)), ACT.Copy)
                nc.vector.tensor_tensor(p89[t][:, lo:hi], h_n9[t][:, lo:hi], h_n8[t][:, lo:hi], ALU.mult)

        def finish(t, lo, hi):
            for h in range(lo // HALF, hi // HALF):
                nc.vector.tensor_tensor(res[h][:, t, :], p67[t][:, half(h)], p89[t][:, half(h)], ALU.subtract)
                nc.sync.dma_start(out_rows[:, t, half(h)], res[h][:, t, :])

        steps = [(0, 0, HALF), (0, HALF, S), (1, 0, S), (2, 0, S), (3, 0, HALF), (3, HALF, S)]
        for k, step in enumerate(steps[:-1]):
            products(*step)
            if k > 0:
                finish(*steps[k - 1])
        finish(*steps[-2])
        products(*steps[-1])
        finish(*steps[-1])

        for h in range(2):
            o_bf = sb(f"o_bf{h}", [P, PACK * HALF], BF16)
            o_w = sb(f"o_w{h}", [P, HALF], U32)
            weave(o_bf, res[h], nc.vector.tensor_copy if h else nc.scalar.copy)
            nc.vector.quantize_mx(out=o_w[:].bitcast(FP8X4), scales=o_s[:, half(h)], in_=o_bf[:])
            nc.sync.dma_start(out_words[:, half(h)], o_w[:].bitcast(I32))
        for r in range(PACK):
            queue = nc.scalar if r % 2 else nc.sync
            queue.dma_start(out_scales[r:16:PACK, :], o_s[r:P:32, :].bitcast(I32))
